import numpy as np
import ml_dtypes


def mxq(x, axis, fmt="e4m3"):
    dtype, down = {"e4m3": (ml_dtypes.float8_e4m3fn, 7), "e5m2": (ml_dtypes.float8_e5m2, 14)}[fmt]
    v = np.moveaxis(np.asarray(x, np.float32).astype(ml_dtypes.bfloat16).astype(np.float64), axis, -1)
    blocks = v.reshape(v.shape[:-1] + (-1, 32))
    amax = np.abs(blocks).max(-1, keepdims=True)
    byte = np.maximum(np.where(amax > 0, np.frexp(amax)[1] - 1 + 127, 0) - down, 1)
    scale = np.exp2(byte - 127.0)
    codes = (blocks / scale).astype(np.float32).astype(dtype).astype(np.float64)
    return np.moveaxis((codes * scale).reshape(v.shape), -1, axis)


WIDE = False


def mx_kscale(k):
    if not WIDE:
        return np.ones(k)
    levels = np.array([10, -10, 5, -5, 0])
    if k % 512:
        return np.exp2(np.random.permutation(np.resize(levels, k // 32))).repeat(32)
    a = np.empty((k // 512, 16))
    for p in range(k // 512):
        a[p, :8] = np.random.permutation(np.resize(levels, 8))
        for g in range(8):
            far = levels[np.abs(levels - a[p, g]) >= 10]
            a[p, g + 8] = far[np.random.randint(len(far))]
    return np.exp2(a.ravel()).repeat(32)


BF16 = ml_dtypes.bfloat16


def bf(x):
    return np.asarray(x, np.float32).astype(BF16)


def f64(x):
    return np.asarray(x).astype(np.float64)


E2M1 = np.array([0.0, 0.5, 1.0, 1.5, 2.0, 3.0, 4.0, 6.0, -0.0, -0.5, -1.0, -1.5, -2.0, -3.0, -4.0, -6.0])


def pack_weight(w, fmt):
    k, n = w.shape
    w = f64(bf(w)).reshape(k // 32, 32, n)
    amax = np.abs(w).max(1)
    if fmt == "e4m3":
        byte = np.frexp(amax)[1] - 1 + 127 - 7
    else:
        mant, ex = np.frexp(amax / 6.0)
        byte = np.where(mant > 0.5, ex, ex - 1) + 127
    byte = np.clip(np.where(amax > 0, byte, 1), 1, 254)
    scaled = (w * np.exp2(127.0 - byte)[:, None, :]).reshape(k, n).astype(np.float32)
    by_word = np.ascontiguousarray(scaled.reshape(k // 512, 128, 4, n).transpose(0, 1, 3, 2))
    if fmt == "e4m3":
        words = by_word.astype(ml_dtypes.float8_e4m3fn).view(np.uint8)
    else:
        c = by_word.astype(ml_dtypes.float4_e2m1fn).view(np.uint8) & 0xF
        words = c[..., 0::2] | (c[..., 1::2] << 4)
    return np.ascontiguousarray(words), np.ascontiguousarray(byte.astype(np.uint8).reshape(k // 512, 16, n))


def unpack_weight(words, scales, fmt):
    g, p, n, _ = words.shape
    if fmt == "e4m3":
        vals = np.ascontiguousarray(words).view(ml_dtypes.float8_e4m3fn).astype(np.float64)
    else:
        nib = np.empty((g, p, n, 4), np.uint8)
        nib[..., 0::2] = words & 0xF
        nib[..., 1::2] = words >> 4
        vals = E2M1[nib]
    vals = vals * np.repeat(np.exp2(scales.astype(np.float64) - 127.0), 8, axis=1)[..., None]
    return vals.transpose(0, 1, 3, 2).reshape(g * 512, n)
def pack4(w):
    words, scales = pack_weight(w, "e2m1")
    return words.reshape(words.shape[0], 128, -1), scales


def unpack4(words, scales):
    return unpack_weight(words.reshape(words.shape[0], 128, -1, 2), scales, "e2m1")


Q, C, B, P, G, S = 512, 1024, 512, 4096, 512, 64


def setup_inputs():
    s, r, t = mx_kscale(C), mx_kscale(B), mx_kscale(P)
    reg = np.random.randint(0, S, P)
    pixels = np.random.standard_normal((C, S))[:, reg] + 0.5 * np.random.standard_normal((C, P))
    proto = np.random.standard_normal((B, S))[:, reg] + 0.5 * np.random.standard_normal((B, P))
    weight = (0.5 + 2.0 * np.random.random(S))[reg]
    mask = (np.random.random((S, G)) < 0.4)[reg] * (0.5 + 0.5 * np.random.random((P, G)))
    mask[:, 0] = 1.0
    area = (weight[:, None] * mask).sum(0) / P
    proto_words, proto_scales = pack4(proto / np.sqrt(B) / r[:, None])
    mask_words, mask_scales = pack4(mask / P / t[:, None])
    return {"embed": bf(1.5 * np.random.standard_normal((Q, C)) * s),
            "pixels": bf(pixels / np.sqrt(C) / s[:, None]),
            "coef": bf(1.5 * np.random.standard_normal((Q, B)) * r),
            "proto_words": proto_words, "proto_scales": proto_scales,
            "weight": bf(weight * t),
            "mask_words": mask_words, "mask_scales": mask_scales,
            "area": bf(area)}


def reference(embed, pixels, coef, proto_words, proto_scales, weight, mask_words, mask_scales, area):
    fine = mxq(f64(embed), 1, "e4m3") @ mxq(f64(pixels), 0, "e4m3")
    coarse = mxq(f64(coef), 1, "e4m3") @ unpack4(proto_words, proto_scales)
    z = fine + coarse
    pred = 1.0 / (1.0 + np.exp(-z))
    pred = pred * f64(weight)
    inter = mxq(pred, 1, "e4m3") @ unpack4(mask_words, mask_scales)
    pred_area = inter[:, :1]
    return 2.0 * inter / (pred_area + f64(area))

@@ -1,0 +1,379 @@
+from contextlib import ExitStack
+
+import concourse.mybir as mybir
+from concourse.masks import make_identity
+
+Q, C, B, P, G = 512, 1024, 512, 4096, 512
+FLOPS = 2 * Q * P * (C + B) + 2 * Q * P * G
+
+F32 = mybir.dt.float32
+BF16 = mybir.dt.bfloat16
+I32 = mybir.dt.int32
+U32 = mybir.dt.uint32
+U8 = mybir.dt.uint8
+FP8X4 = mybir.dt.float8_e4m3fn_x4
+FP4X4 = mybir.dt.float4_e2m1fn_x4
+ACT = mybir.ActivationFunctionType
+ALU = mybir.AluOpType
+
+NG = P // 512
+V_SHARE = [48,48,52,52,52,52,52,52]
+SQUARED = [3]
+
+
+def tile_pairwise_mask_dice_s3_kernel(
+    tc, embed, pixels, coef, proto_words, proto_scales, weight, mask_words, mask_scales, area, out
+):
+    nc = tc.nc
+    with ExitStack() as ctx:
+        keep = ctx.enter_context(tc.tile_pool(name="keep", bufs=1))
+        two = ctx.enter_context(tc.tile_pool(name="two", bufs=2))
+        three = ctx.enter_context(tc.tile_pool(name="three", bufs=3))
+        four = ctx.enter_context(tc.tile_pool(name="four", bufs=4))
+        acc_pool = ctx.enter_context(tc.psum_pool(name="acc", bufs=1))
+        st_pool = ctx.enter_context(tc.psum_pool(name="st", bufs=4))
+
+        ident = keep.tile([128, 128], F32, name="ident", align_bytes=64)
+        coef_raw = keep.tile([128, 4, 512], BF16, name="coef_raw", align_bytes=64)
+        emb_raw = keep.tile([128, 4, 1024], BF16, name="emb_raw", align_bytes=64)
+        proto_raw = keep.tile([128, 2 * P], U8, name="proto_raw", align_bytes=64)
+        proto_wd = keep.tile([128, 2 * P], U8, name="proto_wd", align_bytes=64)
+        pscl_raw = keep.tile([128, P], U8, name="pscl_raw", align_bytes=64)
+        pscl = keep.tile([128, P], U8, name="pscl", align_bytes=64)
+        mask_wd = keep.tile([128, NG, 1024], U8, name="mask_wd", align_bytes=64)
+        mscl = keep.tile([128, NG, 512], U8, name="mscl", align_bytes=64)
+        w_sb = keep.tile([128, NG, 4], BF16, name="w_sb", align_bytes=64)
+        area_b = keep.tile([128, G], BF16, name="area_b", align_bytes=64)
+        warm = keep.tile([128, 1], F32, name="warm")
+
+        coef_grp = keep.tile([128, 2048], BF16, name="coef_grp", align_bytes=64)
+        coef_cd = keep.tile([128, 512], U32, name="coef_cd", align_bytes=64)
+        coef_sc = keep.tile([128, 512], U8, name="coef_sc", align_bytes=64)
+        emb_grp = keep.tile([128, 2, 2048], BF16, name="emb_grp", align_bytes=64)
+        emb_cd = keep.tile([128, 2, 512], U32, name="emb_cd", align_bytes=64)
+        emb_sc = keep.tile([128, 2, 512], U8, name="emb_sc", align_bytes=64)
+
+        px_raw = [keep.tile([128, 2, 4, 512], BF16, name=f"px{g}", align_bytes=64) for g in range(NG)]
+
+        acc = [acc_pool.tile([128, 512], F32, name=f"acc{q}") for q in range(4)]
+
+        def load_px(g):
+            for c in range(2):
+                nc.sync.dma_start(
+                    out=px_raw[g][:, c],
+                    in_=pixels[512 * c : 512 * (c + 1), 512 * g : 512 * (g + 1)].rearrange("(p j) n -> p j n", j=4),
+                )
+
+        def load_proto(b0, b1):
+            nc.sync.dma_start(out=proto_raw[:, b0:b1].bitcast(I32), in_=proto_words[0][:, b0:b1].bitcast(I32))
+
+        ctx.enter_context(tc.manual_schedule())
+
+        nc.vector.memset(pscl_raw[:].bitcast(I32), 0)
+        make_identity(nc, ident[:])
+        nc.vector.memset(warm[:], 0.0)
+        emb_rows = embed.rearrange("(a p) k -> p a k", p=128)
+        load_proto(0, 2048)
+        nc.sync.dma_start(out=coef_raw[:], in_=coef.rearrange("(a p) k -> p a k", p=128))
+        load_proto(2048, 8192)
+        nc.sync.dma_start(out=emb_raw[:, 0:2, :], in_=emb_rows[:, 0:2, :])
+        nc.sync.dma_start(out=emb_raw[:, 2:4, :], in_=emb_rows[:, 2:4, :])
+        load_px(0)
+        load_px(1)
+        load_px(2)
+        nc.sync.dma_start(out=mask_wd[:].bitcast(I32), in_=mask_words.rearrange("g p n -> p g n").bitcast(I32))
+        load_px(3)
+        load_px(4)
+        load_px(5)
+        load_px(6)
+        load_px(7)
+        nc.sync.dma_start(out=area_b[:], in_=area.partition_broadcast(128))
+        for qd in range(4):
+            nc.gpsimd.dma_start(
+                out=pscl_raw[32 * qd : 32 * qd + 4, :].bitcast(I32),
+                in_=proto_scales[0][4 * qd : 4 * qd + 4, :].bitcast(I32),
+            )
+        nc.gpsimd.memset(mscl[:].rearrange("p g n -> p (g n)").bitcast(I32), 0)
+        nc.gpsimd.dma_start(out=w_sb[:], in_=weight.rearrange("(g p t) -> p g t", p=128, t=4))
+        for qd in range(4):
+            nc.gpsimd.dma_start(
+                out=mscl[32 * qd : 32 * qd + 4].bitcast(I32),
+                in_=mask_scales[:, 4 * qd : 4 * qd + 4, :].rearrange("g r n -> r g n").bitcast(I32),
+            )
+        nc.scalar.activation(out=warm[:], in_=warm[:], func=ACT.Sigmoid)
+
+        def turn(raw, a0, word0, dst, copy):
+            bank = st_pool.tile([128, 512], F32, name="st")
+            for a in range(2):
+                words = raw[:, a0 + a, :].bitcast(F32)
+                for u in range(2):
+                    nc.tensor.transpose(
+                        bank[:, 128 * (2 * a + u) : 128 * (2 * a + u + 1)],
+                        words[:, word0 + u : word0 + 256 : 2],
+                        ident[:],
+                    )
+            copy(
+                out=dst[:, 512 * a0 : 512 * (a0 + 2)].bitcast(F32).rearrange("p (a r u) -> p a r u", a=2, u=2),
+                in_=bank[:].rearrange("p (a u r) -> p a r u", a=2, u=2),
+            )
+
+        def permute_words(g):
+            nc.vector.tensor_copy(
+                out=proto_wd[:, 1024 * g : 1024 * (g + 1)].rearrange("p (t m b) -> p t m b", t=4, b=2),
+                in_=proto_raw[:, 1024 * g : 1024 * (g + 1)].rearrange("p (m t b) -> p t m b", t=4, b=2),
+            )
+
+        def permute_scales(g0, g1):
+            nc.vector.tensor_copy(
+                out=pscl[:, 512 * g0 : 512 * g1].rearrange("p (g t m) -> p g t m", t=4, m=128),
+                in_=pscl_raw[:, 512 * g0 : 512 * g1].rearrange("p (g m t) -> p g t m", t=4, m=128),
+            )
+
+        grp = {}
+        px_q = {}
+        sig = {}
+        hgrp = {}
+        h_q = {}
+        zs = {}
+
+        def interleave(copy, g, c, m0, m1):
+            if m1 > m0:
+                copy(
+                    out=grp[g][:, c, :].rearrange("p (t m j) -> p m j t", t=4, j=4)[:, m0:m1],
+                    in_=px_raw[g][:, c].rearrange("p j (m t) -> p m j t", t=4)[:, m0:m1],
+                )
+
+        def start_group(g):
+            grp[g] = two.tile([128, 2, 2048], BF16, name="grp", align_bytes=64)
+            px_q[g] = (
+                three.tile([128, 2, 512], U32, name="pxcd", align_bytes=64),
+                three.tile([128, 2, 512], U8, name="pxsc", align_bytes=64),
+            )
+
+        def quant_px(g, c):
+            codes, scl = px_q[g]
+            nc.vector.quantize_mx(out=codes[:, c, :].bitcast(FP8X4), scales=scl[:, c, :], in_=grp[g][:, c, :])
+
+        def quant_coef():
+            nc.vector.quantize_mx(out=coef_cd[:].bitcast(FP8X4), scales=coef_sc[:], in_=coef_grp[:])
+
+        def quant_emb(c):
+            nc.vector.quantize_mx(out=emb_cd[:, c, :].bitcast(FP8X4), scales=emb_sc[:, c, :], in_=emb_grp[:, c, :])
+
+        def coarse(g, t):
+            zs[g, t] = st_pool.tile([128, 512], F32, name="st")
+            col = 512 * g + 128 * t
+            nc.tensor.matmul_mx(
+                out=zs[g, t][:],
+                lhsT=proto_wd[:, 2 * col : 2 * col + 256].bitcast(FP4X4),
+                lhsT_scale=pscl[:, col : col + 128],
+                rhs=coef_cd[:].bitcast(FP8X4),
+                rhs_scale=coef_sc[:],
+                start=True,
+                stop=False,
+            )
+
+        def fine(g, t):
+            codes, scl = px_q[g]
+            for c in range(2):
+                nc.tensor.matmul_mx(
+                    out=zs[g, t][:],
+                    lhsT=codes[:, c, 128 * t : 128 * (t + 1)].bitcast(FP8X4),
+                    lhsT_scale=scl[:, c, 128 * t : 128 * (t + 1)],
+                    rhs=emb_cd[:, c, :].bitcast(FP8X4),
+                    rhs_scale=emb_sc[:, c, :],
+                    start=False,
+                    stop=(c == 1),
+                )
+
+        def sigmoid(g, t, q0=0, q1=512):
+            if t == 0:
+                sig[g] = two.tile([128, 4, 512], F32, name="sig", align_bytes=64)
+            nc.scalar.activation(out=sig[g][:, t, q0:q1], in_=zs[g, t][:, q0:q1], func=ACT.Sigmoid)
+
+        def start_h(g):
+            hgrp[g] = two.tile([128, 2048], BF16, name="hgrp", align_bytes=64)
+            h_q[g] = (
+                three.tile([128, 512], U32, name="hcd", align_bytes=64),
+                three.tile([128, 512], U8, name="hsc", align_bytes=64),
+            )
+
+        def weigh(g, q0, q1):
+            n = (q1 - q0) // 2
+            nc.vector.tensor_tensor(
+                out=hgrp[g][:, 4 * q0 : 4 * q1].rearrange("p (c i t) -> p c t i", i=2, t=4),
+                in0=sig[g][:, :, q0:q1].rearrange("p t (c i) -> p c t i", i=2),
+                in1=w_sb[:, g, :].unsqueeze(1).unsqueeze(3).to_broadcast([128, n, 4, 2]),
+                op=ALU.mult,
+            )
+
+        def quant_h(g, q0, q1):
+            cd, sc = h_q[g]
+            nc.vector.quantize_mx(
+                out=cd[:, q0:q1].bitcast(FP8X4), scales=sc[:, q0:q1], in_=hgrp[g][:, 4 * q0 : 4 * q1]
+            )
+
+        def stage2(g, q):
+            cd, sc = h_q[g]
+            nc.tensor.matmul_mx(
+                out=acc[q][:],
+                lhsT=cd[:, 128 * q : 128 * (q + 1)].bitcast(FP8X4),
+                lhsT_scale=sc[:, 128 * q : 128 * (q + 1)],
+                rhs=mask_wd[:, g, :].bitcast(FP4X4),
+                rhs_scale=mscl[:, g, :],
+                start=(g == 0),
+                stop=(g == NG - 1),
+            )
+
+        v_copy, s_copy = nc.vector.tensor_copy, nc.scalar.copy
+
+        permute_words(0)
+        permute_words(1)
+        turn(coef_raw, 0, 0, coef_grp, s_copy)
+        turn(coef_raw, 2, 0, coef_grp, s_copy)
+        permute_words(2)
+        permute_words(3)
+        permute_scales(0, 2)
+        permute_words(4)
+        permute_words(5)
+        quant_coef()
+        turn(emb_raw, 0, 0, emb_grp[:, 0, :], s_copy)
+        turn(emb_raw, 0, 256, emb_grp[:, 1, :], s_copy)
+        turn(emb_raw, 2, 0, emb_grp[:, 0, :], s_copy)
+        turn(emb_raw, 2, 256, emb_grp[:, 1, :], s_copy)
+        for t in range(4):
+            coarse(0, t)
+        permute_words(6)
+        permute_words(7)
+        permute_scales(2, 4)
+        permute_scales(4, 6)
+        permute_scales(6, 8)
+        start_group(0)
+        interleave(v_copy, 0, 0, 0, V_SHARE[0])
+        interleave(s_copy, 0, 0, V_SHARE[0], 128)
+        quant_emb(0)
+        quant_emb(1)
+        interleave(v_copy, 0, 1, 0, V_SHARE[0])
+        interleave(s_copy, 0, 1, V_SHARE[0], 128)
+        quant_px(0, 0)
+        start_group(1)
+        interleave(v_copy, 1, 0, 0, V_SHARE[1])
+        interleave(s_copy, 1, 0, V_SHARE[1], 128)
+        quant_px(0, 1)
+        interleave(v_copy, 1, 1, 0, V_SHARE[1])
+        interleave(s_copy, 1, 1, V_SHARE[1], 128)
+
+        for i in range(NG):
+            nxt = i + 2
+            if nxt < NG:
+                start_group(nxt)
+            if i + 1 < NG:
+                quant_px(i + 1, 0)
+                quant_px(i + 1, 1)
+            if i >= 1:
+                start_h(i - 1)
+                weigh(i - 1, 0, 256)
+                weigh(i - 1, 256, 512)
+            if nxt < NG:
+                interleave(v_copy, nxt, 0, 0, V_SHARE[nxt])
+            if i >= 1:
+                quant_h(i - 1, 0, 256)
+            if nxt < NG:
+                interleave(v_copy, nxt, 1, 0, V_SHARE[nxt])
+            if i >= 1:
+                quant_h(i - 1, 256, 512)
+
+            last = i == NG - 1
+            for t in range(4):
+                if i > 0:
+                    coarse(i, t)
+                fine(i, t)
+                if last and t == 3:
+                    for q in range(4):
+                        sigmoid(i, t, 128 * q, 128 * (q + 1))
+                else:
+                    sigmoid(i, t)
+                if nxt < NG:
+                    c, half = t // 2, t % 2
+                    v = V_SHARE[nxt]
+                    mid = v + (128 - v) // 2
+                    lo, hi = ((v, mid), (mid, 128))[half]
+                    interleave(s_copy, nxt, c, lo, hi)
+                if t == 0 and i >= 2 and not last:
+                    for q in range(4):
+                        stage2(i - 2, q)
+
+        g = NG - 1
+        nc.scalar.activation(out=warm[:], in_=warm[:], func=ACT.Abs_reciprocal_sqrt)
+        for k in (g - 2, g - 1):
+            for q in range(4):
+                stage2(k, q)
+        start_h(g)
+        weigh(g, 0, 128)
+        weigh(g, 128, 256)
+        quant_h(g, 0, 128)
+        weigh(g, 256, 384)
+        quant_h(g, 128, 256)
+        weigh(g, 384, 512)
+        quant_h(g, 256, 384)
+        quant_h(g, 384, 512)
+        for q in range(4):
+            stage2(g, q)
+
+        num = {}
+        inv = {}
+        i0s = {}
+        sgn = {}
+
+        def scalar_part(q):
+            i0 = four.tile([128, 1], F32, name="i0")
+            nc.scalar.copy(out=i0[:], in_=acc[q][:, 0:1])
+            r1 = two.tile([128, 512], F32, name="r1")
+            nc.scalar.activation(out=r1[:], in_=area_b[:], func=ACT.Abs_reciprocal_sqrt, bias=i0[:])
+            r2 = four.tile([128, 512], F32, name="r2")
+            nc.scalar.activation(out=r2[:], in_=r1[:], func=ACT.Square)
+            if q in SQUARED:
+                r4 = two.tile([128, 512], F32, name="r4")
+                nc.scalar.activation(out=r4[:], in_=r2[:], func=ACT.Square)
+                r2 = r4
+            inv[q] = r2
+            i0s[q] = i0
+
+        def vector_first(q):
+            n = four.tile([128, 512], F32, name="num")
+            num[q] = n
+            if q in SQUARED:
+                nc.vector.scalar_tensor_tensor(
+                    out=n[:], in0=area_b[:], scalar=i0s[q][:], in1=acc[q][:], op0=ALU.add, op1=ALU.mult
+                )
+            else:
+                m0 = four.tile([128, 1], F32, name="m0")
+                nc.vector.tensor_scalar(
+                    out=m0[:], in0=i0s[q][:], scalar1=-1.0, scalar2=None, op0=ALU.mult
+                )
+                s = two.tile([128, 512], F32, name="sgn")
+                nc.vector.tensor_scalar(
+                    out=s[:], in0=area_b[:], scalar1=m0[:], scalar2=0.5, op0=ALU.is_ge, op1=ALU.subtract
+                )
+                sgn[q] = s
+
+        def vector_second(q):
+            res = four.tile([128, 512], F32, name="res")
+            if q in SQUARED:
+                nc.vector.scalar_tensor_tensor(
+                    out=res[:], in0=num[q][:], scalar=2.0, in1=inv[q][:], op0=ALU.mult, op1=ALU.mult
+                )
+            else:
+                n = num[q]
+                nc.vector.scalar_tensor_tensor(
+                    out=n[:], in0=acc[q][:], scalar=4.0, in1=inv[q][:], op0=ALU.mult, op1=ALU.mult
+                )
+                nc.vector.tensor_tensor(out=res[:], in0=n[:], in1=sgn[q][:], op=ALU.mult)
+            nc.sync.dma_start(out=out[128 * q : 128 * (q + 1), :], in_=res[:])
+
+        for q in range(4):
+            scalar_part(q)
+            vector_first(q)
+            if q >= 1:
+                vector_second(q - 1)
+        vector_second(3)

@@ -17,8 +17,11 @@ ACT = mybir.ActivationFunctionType
 ALU = mybir.AluOpType
 
 NG = P // 512
-V_SHARE = [48,48,52,52,52,52,52,52]
-SQUARED = [3]
+V_SHARE = [64,72,88,32,32,32,32,32]
+
+GFIRST = 3
+T1 = 1
+G_RUNS = ((0, 256), (256, 384))
 
 
 def tile_pairwise_mask_dice_s3_kernel(
@@ -31,7 +34,8 @@ def tile_pairwise_mask_dice_s3_kernel(
         three = ctx.enter_context(tc.tile_pool(name="three", bufs=3))
         four = ctx.enter_context(tc.tile_pool(name="four", bufs=4))
         acc_pool = ctx.enter_context(tc.psum_pool(name="acc", bufs=1))
-        st_pool = ctx.enter_context(tc.psum_pool(name="st", bufs=4))
+        w_pool = ctx.enter_context(tc.psum_pool(name="wp", bufs=1))
+        st_pool = ctx.enter_context(tc.psum_pool(name="st", bufs=3))
 
         ident = keep.tile([128, 128], F32, name="ident", align_bytes=64)
         coef_raw = keep.tile([128, 4, 512], BF16, name="coef_raw", align_bytes=64)
@@ -44,6 +48,9 @@ def tile_pairwise_mask_dice_s3_kernel(
         mscl = keep.tile([128, NG, 512], U8, name="mscl", align_bytes=64)
         w_sb = keep.tile([128, NG, 4], BF16, name="w_sb", align_bytes=64)
         area_b = keep.tile([128, G], BF16, name="area_b", align_bytes=64)
+        w_pad = keep.tile([128, 128], F32, name="w_pad", align_bytes=64)
+        w_turn = keep.tile([128, 128], F32, name="w_turn", align_bytes=64)
+        w_ps = w_pool.tile([128, 128], F32, name="w_ps")
         warm = keep.tile([128, 1], F32, name="warm")
 
         coef_grp = keep.tile([128, 2048], BF16, name="coef_grp", align_bytes=64)
@@ -72,34 +79,36 @@ def tile_pairwise_mask_dice_s3_kernel(
         nc.vector.memset(pscl_raw[:].bitcast(I32), 0)
         make_identity(nc, ident[:])
         nc.vector.memset(warm[:], 0.0)
-        emb_rows = embed.rearrange("(a p) k -> p a k", p=128)
+        nc.gpsimd.memset(w_pad[:], 0.0)
+        nc.gpsimd.memset(mscl[:].rearrange("p g n -> p (g n)").bitcast(I32), 0)
+        emb_rows = embed.rearrange("(p a) k -> p a k", a=4)
+        load_proto(2048, 4096)
         load_proto(0, 2048)
-        nc.sync.dma_start(out=coef_raw[:], in_=coef.rearrange("(a p) k -> p a k", p=128))
-        load_proto(2048, 8192)
+        nc.sync.dma_start(out=coef_raw[:], in_=coef.rearrange("(p a) k -> p a k", a=4))
+        for qd in range(4):
+            nc.sync.dma_start(
+                out=pscl_raw[32 * qd : 32 * qd + 4, :].bitcast(I32),
+                in_=proto_scales[0][4 * qd : 4 * qd + 4, :].bitcast(I32),
+            )
+        load_proto(4096, 8192)
         nc.sync.dma_start(out=emb_raw[:, 0:2, :], in_=emb_rows[:, 0:2, :])
         nc.sync.dma_start(out=emb_raw[:, 2:4, :], in_=emb_rows[:, 2:4, :])
+        nc.sync.dma_start(out=w_sb[:], in_=weight.rearrange("(g p t) -> p g t", p=128, t=4))
         load_px(0)
         load_px(1)
         load_px(2)
-        nc.sync.dma_start(out=mask_wd[:].bitcast(I32), in_=mask_words.rearrange("g p n -> p g n").bitcast(I32))
         load_px(3)
+        nc.sync.dma_start(out=mask_wd[:].bitcast(I32), in_=mask_words.rearrange("g p n -> p g n").bitcast(I32))
+        for qd in range(4):
+            nc.sync.dma_start(
+                out=mscl[32 * qd : 32 * qd + 4].bitcast(I32),
+                in_=mask_scales[:, 4 * qd : 4 * qd + 4, :].rearrange("g r n -> r g n").bitcast(I32),
+            )
         load_px(4)
         load_px(5)
         load_px(6)
         load_px(7)
         nc.sync.dma_start(out=area_b[:], in_=area.partition_broadcast(128))
-        for qd in range(4):
-            nc.gpsimd.dma_start(
-                out=pscl_raw[32 * qd : 32 * qd + 4, :].bitcast(I32),
-                in_=proto_scales[0][4 * qd : 4 * qd + 4, :].bitcast(I32),
-            )
-        nc.gpsimd.memset(mscl[:].rearrange("p g n -> p (g n)").bitcast(I32), 0)
-        nc.gpsimd.dma_start(out=w_sb[:], in_=weight.rearrange("(g p t) -> p g t", p=128, t=4))
-        for qd in range(4):
-            nc.gpsimd.dma_start(
-                out=mscl[32 * qd : 32 * qd + 4].bitcast(I32),
-                in_=mask_scales[:, 4 * qd : 4 * qd + 4, :].rearrange("g r n -> r g n").bitcast(I32),
-            )
         nc.scalar.activation(out=warm[:], in_=warm[:], func=ACT.Sigmoid)
 
         def turn(raw, a0, word0, dst, copy):
@@ -129,7 +138,15 @@ def tile_pairwise_mask_dice_s3_kernel(
                 in_=pscl_raw[:, 512 * g0 : 512 * g1].rearrange("p (g m t) -> p g t m", t=4, m=128),
             )
 
+        def place_weights():
+            nc.scalar.copy(out=w_pad[:, 0 : 4 * NG], in_=w_sb[:].rearrange("p g t -> p (g t)"))
+            bank = st_pool.tile([128, 512], F32, name="st")
+            nc.tensor.transpose(bank[:, 0:128], w_pad[:], ident[:])
+            nc.scalar.copy(out=w_turn[:], in_=bank[:, 0:128])
+            nc.tensor.transpose(w_ps[:], w_turn[:], ident[:])
+
         grp = {}
+        grp_g = {}
         px_q = {}
         sig = {}
         hgrp = {}
@@ -138,13 +155,34 @@ def tile_pairwise_mask_dice_s3_kernel(
 
         def interleave(copy, g, c, m0, m1):
             if m1 > m0:
+                nt = 4 if c == 0 else T1
                 copy(
-                    out=grp[g][:, c, :].rearrange("p (t m j) -> p m j t", t=4, j=4)[:, m0:m1],
-                    in_=px_raw[g][:, c].rearrange("p j (m t) -> p m j t", t=4)[:, m0:m1],
+                    out=grp[g][:, 2048 * c : 2048 * c + 512 * nt].rearrange("p (t m j) -> p m j t", t=nt, j=4)[:, m0:m1],
+                    in_=px_raw[g][:, c].rearrange("p j (m t) -> p m j t", t=4)[:, m0:m1, :, 0:nt],
+                )
+
+        def gpsimd_share(g):
+            grp_g[g] = keep.tile([128, 512 * (4 - T1)], BF16, name="grp_g", align_bytes=64)
+            nc.gpsimd.tensor_scalar(
+                out=grp_g[g][:].rearrange("p (t m j) -> p m j t", t=4 - T1, j=4),
+                in0=px_raw[g][:, 1].rearrange("p j (m t) -> p m j t", t=4)[:, :, :, T1:4],
+                scalar1=1.0,
+                scalar2=0.0,
+                op0=ALU.mult,
+                op1=ALU.add,
+            )
+
+        def alone(copy, g, m0, m1):
+            if m0 == 0:
+                grp_g[g] = keep.tile([128, 512 * (4 - T1)], BF16, name="grp_g", align_bytes=64)
+            if m1 > m0:
+                copy(
+                    out=grp_g[g][:].rearrange("p (t m j) -> p m j t", t=4 - T1, j=4)[:, m0:m1],
+                    in_=px_raw[g][:, 1].rearrange("p j (m t) -> p m j t", t=4)[:, m0:m1, :, T1:4],
                 )
 
         def start_group(g):
-            grp[g] = two.tile([128, 2, 2048], BF16, name="grp", align_bytes=64)
+            grp[g] = two.tile([128, 2048 + 512 * T1], BF16, name="grp", align_bytes=64)
             px_q[g] = (
                 three.tile([128, 2, 512], U32, name="pxcd", align_bytes=64),
                 three.tile([128, 2, 512], U8, name="pxsc", align_bytes=64),
@@ -152,7 +190,19 @@ def tile_pairwise_mask_dice_s3_kernel(
 
         def quant_px(g, c):
             codes, scl = px_q[g]
-            nc.vector.quantize_mx(out=codes[:, c, :].bitcast(FP8X4), scales=scl[:, c, :], in_=grp[g][:, c, :])
+            n = 512 if c == 0 else 128 * T1
+            nc.vector.quantize_mx(
+                out=codes[:, c, 0:n].bitcast(FP8X4),
+                scales=scl[:, c, 0:n],
+                in_=grp[g][:, 2048 * c : 2048 * c + 4 * n],
+            )
+            if c == 1:
+                for a, b in G_RUNS:
+                    nc.vector.quantize_mx(
+                        out=codes[:, 1, n + a : n + b].bitcast(FP8X4),
+                        scales=scl[:, 1, n + a : n + b],
+                        in_=grp_g[g][:, 4 * a : 4 * b],
+                    )
 
         def quant_coef():
             nc.vector.quantize_mx(out=coef_cd[:].bitcast(FP8X4), scales=coef_sc[:], in_=coef_grp[:])
@@ -203,7 +253,7 @@ def tile_pairwise_mask_dice_s3_kernel(
             nc.vector.tensor_tensor(
                 out=hgrp[g][:, 4 * q0 : 4 * q1].rearrange("p (c i t) -> p c t i", i=2, t=4),
                 in0=sig[g][:, :, q0:q1].rearrange("p t (c i) -> p c t i", i=2),
-                in1=w_sb[:, g, :].unsqueeze(1).unsqueeze(3).to_broadcast([128, n, 4, 2]),
+                in1=w_ps[:, 4 * g : 4 * g + 4].unsqueeze(1).unsqueeze(3).to_broadcast([128, n, 4, 2]),
                 op=ALU.mult,
             )
 
@@ -227,40 +277,44 @@ def tile_pairwise_mask_dice_s3_kernel(
 
         v_copy, s_copy = nc.vector.tensor_copy, nc.scalar.copy
 
+        turn(coef_raw, 0, 0, coef_grp, s_copy)
         permute_words(0)
         permute_words(1)
-        turn(coef_raw, 0, 0, coef_grp, s_copy)
-        turn(coef_raw, 2, 0, coef_grp, s_copy)
         permute_words(2)
         permute_words(3)
+        turn(coef_raw, 2, 0, coef_grp, s_copy)
         permute_scales(0, 2)
         permute_words(4)
-        permute_words(5)
         quant_coef()
         turn(emb_raw, 0, 0, emb_grp[:, 0, :], s_copy)
-        turn(emb_raw, 0, 256, emb_grp[:, 1, :], s_copy)
+        turn(emb_raw, 0, 256, emb_grp[:, 1, :], v_copy)
         turn(emb_raw, 2, 0, emb_grp[:, 0, :], s_copy)
         turn(emb_raw, 2, 256, emb_grp[:, 1, :], s_copy)
-        for t in range(4):
-            coarse(0, t)
         permute_words(6)
         permute_words(7)
         permute_scales(2, 4)
-        permute_scales(4, 6)
         permute_scales(6, 8)
+        place_weights()
+        for t in range(3):
+            coarse(0, t)
         start_group(0)
-        interleave(v_copy, 0, 0, 0, V_SHARE[0])
         interleave(s_copy, 0, 0, V_SHARE[0], 128)
+        permute_words(5)
+        interleave(v_copy, 0, 0, 0, V_SHARE[0])
         quant_emb(0)
+        quant_px(0, 0)
         quant_emb(1)
         interleave(v_copy, 0, 1, 0, V_SHARE[0])
         interleave(s_copy, 0, 1, V_SHARE[0], 128)
-        quant_px(0, 0)
+        alone(v_copy, 0, 0, V_SHARE[0])
+        alone(s_copy, 0, V_SHARE[0], 128)
         start_group(1)
         interleave(v_copy, 1, 0, 0, V_SHARE[1])
         interleave(s_copy, 1, 0, V_SHARE[1], 128)
         quant_px(0, 1)
         interleave(v_copy, 1, 1, 0, V_SHARE[1])
+        alone(v_copy, 1, 0, V_SHARE[1])
+        alone(s_copy, 1, V_SHARE[1], 128)
         interleave(s_copy, 1, 1, V_SHARE[1], 128)
 
         for i in range(NG):
@@ -270,6 +324,8 @@ def tile_pairwise_mask_dice_s3_kernel(
             if i + 1 < NG:
                 quant_px(i + 1, 0)
                 quant_px(i + 1, 1)
+            if GFIRST <= nxt < NG:
+                gpsimd_share(nxt)
             if i >= 1:
                 start_h(i - 1)
                 weigh(i - 1, 0, 256)
@@ -280,12 +336,15 @@ def tile_pairwise_mask_dice_s3_kernel(
                 quant_h(i - 1, 0, 256)
             if nxt < NG:
                 interleave(v_copy, nxt, 1, 0, V_SHARE[nxt])
+                if nxt < GFIRST:
+                    alone(v_copy, nxt, 0, V_SHARE[nxt])
             if i >= 1:
                 quant_h(i - 1, 256, 512)
-
+            if i == 0:
+                permute_scales(4, 6)
             last = i == NG - 1
             for t in range(4):
-                if i > 0:
+                if i > 0 or t == 3:
                     coarse(i, t)
                 fine(i, t)
                 if last and t == 3:
@@ -299,6 +358,8 @@ def tile_pairwise_mask_dice_s3_kernel(
                     mid = v + (128 - v) // 2
                     lo, hi = ((v, mid), (mid, 128))[half]
                     interleave(s_copy, nxt, c, lo, hi)
+                    if t == 3 and nxt < GFIRST:
+                        alone(s_copy, nxt, v, 128)
                 if t == 0 and i >= 2 and not last:
                     for q in range(4):
                         stage2(i - 2, q)
@@ -309,71 +370,89 @@ def tile_pairwise_mask_dice_s3_kernel(
             for q in range(4):
                 stage2(k, q)
         start_h(g)
-        weigh(g, 0, 128)
-        weigh(g, 128, 256)
-        quant_h(g, 0, 128)
-        weigh(g, 256, 384)
-        quant_h(g, 128, 256)
-        weigh(g, 384, 512)
-        quant_h(g, 256, 384)
-        quant_h(g, 384, 512)
-        for q in range(4):
-            stage2(g, q)
+        for q0 in (0, 256):
+            n = 128
+            nc.vector.tensor_tensor(
+                out=hgrp[g][:, 4 * q0 : 4 * q0 + 1024].rearrange("p (c i t) -> p c t i", i=2, t=4)[:, :, 0:3],
+                in0=sig[g][:, 0:3, q0 : q0 + 256].rearrange("p t (c i) -> p c t i", i=2),
+                in1=w_ps[:, 4 * g : 4 * g + 3].unsqueeze(1).unsqueeze(3).to_broadcast([128, n, 3, 2]),
+                op=ALU.mult,
+            )
 
+        def weigh_last(q):
+            nc.vector.tensor_scalar(
+                out=hgrp[g][:, 512 * q : 512 * (q + 1)].rearrange("p (c t) -> p c t", t=4)[:, :, 3],
+                in0=sig[g][:, 3, 128 * q : 128 * (q + 1)],
+                scalar1=w_pad[:, 4 * g + 3 : 4 * g + 4],
+                scalar2=None,
+                op0=ALU.mult,
+            )
+
+        m0s = {}
+        sgn = {}
         num = {}
         inv = {}
-        i0s = {}
-        sgn = {}
 
-        def scalar_part(q):
-            i0 = four.tile([128, 1], F32, name="i0")
-            nc.scalar.copy(out=i0[:], in_=acc[q][:, 0:1])
+        def minus_area(q):
+            m0s[q] = four.tile([128, 1], F32, name="m0")
+            nc.vector.tensor_scalar(out=m0s[q][:], in0=acc[q][:, 0:1], scalar1=-1.0, scalar2=None, op0=ALU.mult)
+
+        def sign(engine, q):
+            sgn[q] = four.tile([128, 512], F32, name="sgn")
+            engine.tensor_scalar(
+                out=sgn[q][:], in0=area_b[:], scalar1=m0s[q][:], scalar2=0.5, op0=ALU.is_ge, op1=ALU.subtract
+            )
+
+        def root(q):
             r1 = two.tile([128, 512], F32, name="r1")
-            nc.scalar.activation(out=r1[:], in_=area_b[:], func=ACT.Abs_reciprocal_sqrt, bias=i0[:])
+            nc.scalar.activation(
+                out=r1[:], in_=area_b[:], func=ACT.Abs_reciprocal_sqrt, bias=m0s[q][:], scale=-1.0
+            )
+            inv[q] = r1
+
+        def square(q):
             r2 = four.tile([128, 512], F32, name="r2")
-            nc.scalar.activation(out=r2[:], in_=r1[:], func=ACT.Square)
-            if q in SQUARED:
-                r4 = two.tile([128, 512], F32, name="r4")
-                nc.scalar.activation(out=r4[:], in_=r2[:], func=ACT.Square)
-                r2 = r4
+            nc.scalar.activation(out=r2[:], in_=inv[q][:], func=ACT.Square)
             inv[q] = r2
-            i0s[q] = i0
 
-        def vector_first(q):
-            n = four.tile([128, 512], F32, name="num")
-            num[q] = n
-            if q in SQUARED:
-                nc.vector.scalar_tensor_tensor(
-                    out=n[:], in0=area_b[:], scalar=i0s[q][:], in1=acc[q][:], op0=ALU.add, op1=ALU.mult
-                )
-            else:
-                m0 = four.tile([128, 1], F32, name="m0")
-                nc.vector.tensor_scalar(
-                    out=m0[:], in0=i0s[q][:], scalar1=-1.0, scalar2=None, op0=ALU.mult
-                )
-                s = two.tile([128, 512], F32, name="sgn")
-                nc.vector.tensor_scalar(
-                    out=s[:], in0=area_b[:], scalar1=m0[:], scalar2=0.5, op0=ALU.is_ge, op1=ALU.subtract
-                )
-                sgn[q] = s
+        def signed(q):
+            num[q] = four.tile([128, 512], F32, name="num")
+            nc.vector.scalar_tensor_tensor(
+                out=num[q][:], in0=acc[q][:], scalar=4.0, in1=sgn[q][:], op0=ALU.mult, op1=ALU.mult
+            )
 
-        def vector_second(q):
+        def finish(q):
             res = four.tile([128, 512], F32, name="res")
-            if q in SQUARED:
-                nc.vector.scalar_tensor_tensor(
-                    out=res[:], in0=num[q][:], scalar=2.0, in1=inv[q][:], op0=ALU.mult, op1=ALU.mult
-                )
-            else:
-                n = num[q]
-                nc.vector.scalar_tensor_tensor(
-                    out=n[:], in0=acc[q][:], scalar=4.0, in1=inv[q][:], op0=ALU.mult, op1=ALU.mult
-                )
-                nc.vector.tensor_tensor(out=res[:], in0=n[:], in1=sgn[q][:], op=ALU.mult)
-            nc.sync.dma_start(out=out[128 * q : 128 * (q + 1), :], in_=res[:])
+            nc.vector.tensor_tensor(out=res[:], in0=num[q][:], in1=inv[q][:], op=ALU.mult)
+            nc.sync.dma_start(out=out.rearrange("(p a) n -> a p n", a=4)[q], in_=res[:])
 
+        weigh_last(0)
+        weigh_last(1)
+        quant_h(g, 0, 128)
+        stage2(g, 0)
+        weigh_last(2)
+        quant_h(g, 128, 256)
+        stage2(g, 1)
+        weigh_last(3)
+        quant_h(g, 256, 384)
+        stage2(g, 2)
+        minus_area(0)
+        quant_h(g, 384, 512)
+        stage2(g, 3)
         for q in range(4):
-            scalar_part(q)
-            vector_first(q)
             if q >= 1:
-                vector_second(q - 1)
-        vector_second(3)
+                minus_area(q)
+            root(q)
+            square(q)
+        sign(nc.vector, 0)
+        sign(nc.vector, 1)
+        sign(nc.gpsimd, 2)
+        sign(nc.gpsimd, 3)
+        signed(0)
+        signed(1)
+        finish(0)
+        signed(2)
+        finish(1)
+        signed(3)
+        finish(2)
+        finish(3)

from contextlib import ExitStack

import concourse.mybir as mybir
from concourse.masks import make_identity

Q, C, B, P, G = 512, 1024, 512, 4096, 512
FLOPS = 2 * Q * P * (C + B) + 2 * Q * P * G

F32 = mybir.dt.float32
BF16 = mybir.dt.bfloat16
I32 = mybir.dt.int32
U32 = mybir.dt.uint32
U8 = mybir.dt.uint8
FP8X4 = mybir.dt.float8_e4m3fn_x4
FP4X4 = mybir.dt.float4_e2m1fn_x4
ACT = mybir.ActivationFunctionType
ALU = mybir.AluOpType

NG = P // 512
V_SHARE = [64,72,88,32,32,32,32,32]

GFIRST = 3
T1 = 1
G_RUNS = ((0, 256), (256, 384))


def tile_pairwise_mask_dice_s3_kernel(
    tc, embed, pixels, coef, proto_words, proto_scales, weight, mask_words, mask_scales, area, out
):
    nc = tc.nc
    with ExitStack() as ctx:
        keep = ctx.enter_context(tc.tile_pool(name="keep", bufs=1))
        two = ctx.enter_context(tc.tile_pool(name="two", bufs=2))
        three = ctx.enter_context(tc.tile_pool(name="three", bufs=3))
        four = ctx.enter_context(tc.tile_pool(name="four", bufs=4))
        acc_pool = ctx.enter_context(tc.psum_pool(name="acc", bufs=1))
        w_pool = ctx.enter_context(tc.psum_pool(name="wp", bufs=1))
        st_pool = ctx.enter_context(tc.psum_pool(name="st", bufs=3))

        ident = keep.tile([128, 128], F32, name="ident", align_bytes=64)
        coef_raw = keep.tile([128, 4, 512], BF16, name="coef_raw", align_bytes=64)
        emb_raw = keep.tile([128, 4, 1024], BF16, name="emb_raw", align_bytes=64)
        proto_raw = keep.tile([128, 2 * P], U8, name="proto_raw", align_bytes=64)
        proto_wd = keep.tile([128, 2 * P], U8, name="proto_wd", align_bytes=64)
        pscl_raw = keep.tile([128, P], U8, name="pscl_raw", align_bytes=64)
        pscl = keep.tile([128, P], U8, name="pscl", align_bytes=64)
        mask_wd = keep.tile([128, NG, 1024], U8, name="mask_wd", align_bytes=64)
        mscl = keep.tile([128, NG, 512], U8, name="mscl", align_bytes=64)
        w_sb = keep.tile([128, NG, 4], BF16, name="w_sb", align_bytes=64)
        area_b = keep.tile([128, G], BF16, name="area_b", align_bytes=64)
        w_pad = keep.tile([128, 128], F32, name="w_pad", align_bytes=64)
        w_turn = keep.tile([128, 128], F32, name="w_turn", align_bytes=64)
        w_ps = w_pool.tile([128, 128], F32, name="w_ps")
        warm = keep.tile([128, 1], F32, name="warm")

        coef_grp = keep.tile([128, 2048], BF16, name="coef_grp", align_bytes=64)
        coef_cd = keep.tile([128, 512], U32, name="coef_cd", align_bytes=64)
        coef_sc = keep.tile([128, 512], U8, name="coef_sc", align_bytes=64)
        emb_grp = keep.tile([128, 2, 2048], BF16, name="emb_grp", align_bytes=64)
        emb_cd = keep.tile([128, 2, 512], U32, name="emb_cd", align_bytes=64)
        emb_sc = keep.tile([128, 2, 512], U8, name="emb_sc", align_bytes=64)

        px_raw = [keep.tile([128, 2, 4, 512], BF16, name=f"px{g}", align_bytes=64) for g in range(NG)]

        acc = [acc_pool.tile([128, 512], F32, name=f"acc{q}") for q in range(4)]

        def load_px(g):
            for c in range(2):
                nc.sync.dma_start(
                    out=px_raw[g][:, c],
                    in_=pixels[512 * c : 512 * (c + 1), 512 * g : 512 * (g + 1)].rearrange("(p j) n -> p j n", j=4),
                )

        def load_proto(b0, b1):
            nc.sync.dma_start(out=proto_raw[:, b0:b1].bitcast(I32), in_=proto_words[0][:, b0:b1].bitcast(I32))

        ctx.enter_context(tc.manual_schedule())

        nc.vector.memset(pscl_raw[:].bitcast(I32), 0)
        make_identity(nc, ident[:])
        nc.vector.memset(warm[:], 0.0)
        nc.gpsimd.memset(w_pad[:], 0.0)
        nc.gpsimd.memset(mscl[:].rearrange("p g n -> p (g n)").bitcast(I32), 0)
        emb_rows = embed.rearrange("(p a) k -> p a k", a=4)
        load_proto(2048, 4096)
        load_proto(0, 2048)
        nc.sync.dma_start(out=coef_raw[:], in_=coef.rearrange("(p a) k -> p a k", a=4))
        for qd in range(4):
            nc.sync.dma_start(
                out=pscl_raw[32 * qd : 32 * qd + 4, :].bitcast(I32),
                in_=proto_scales[0][4 * qd : 4 * qd + 4, :].bitcast(I32),
            )
        load_proto(4096, 8192)
        nc.sync.dma_start(out=emb_raw[:, 0:2, :], in_=emb_rows[:, 0:2, :])
        nc.sync.dma_start(out=emb_raw[:, 2:4, :], in_=emb_rows[:, 2:4, :])
        nc.sync.dma_start(out=w_sb[:], in_=weight.rearrange("(g p t) -> p g t", p=128, t=4))
        load_px(0)
        load_px(1)
        load_px(2)
        load_px(3)
        nc.sync.dma_start(out=mask_wd[:].bitcast(I32), in_=mask_words.rearrange("g p n -> p g n").bitcast(I32))
        for qd in range(4):
            nc.sync.dma_start(
                out=mscl[32 * qd : 32 * qd + 4].bitcast(I32),
                in_=mask_scales[:, 4 * qd : 4 * qd + 4, :].rearrange("g r n -> r g n").bitcast(I32),
            )
        load_px(4)
        load_px(5)
        load_px(6)
        load_px(7)
        nc.sync.dma_start(out=area_b[:], in_=area.partition_broadcast(128))
        nc.scalar.activation(out=warm[:], in_=warm[:], func=ACT.Sigmoid)

        def turn(raw, a0, word0, dst, copy):
            bank = st_pool.tile([128, 512], F32, name="st")
            for a in range(2):
                words = raw[:, a0 + a, :].bitcast(F32)
                for u in range(2):
                    nc.tensor.transpose(
                        bank[:, 128 * (2 * a + u) : 128 * (2 * a + u + 1)],
                        words[:, word0 + u : word0 + 256 : 2],
                        ident[:],
                    )
            copy(
                out=dst[:, 512 * a0 : 512 * (a0 + 2)].bitcast(F32).rearrange("p (a r u) -> p a r u", a=2, u=2),
                in_=bank[:].rearrange("p (a u r) -> p a r u", a=2, u=2),
            )

        def permute_words(g):
            nc.vector.tensor_copy(
                out=proto_wd[:, 1024 * g : 1024 * (g + 1)].rearrange("p (t m b) -> p t m b", t=4, b=2),
                in_=proto_raw[:, 1024 * g : 1024 * (g + 1)].rearrange("p (m t b) -> p t m b", t=4, b=2),
            )

        def permute_scales(g0, g1):
            nc.vector.tensor_copy(
                out=pscl[:, 512 * g0 : 512 * g1].rearrange("p (g t m) -> p g t m", t=4, m=128),
                in_=pscl_raw[:, 512 * g0 : 512 * g1].rearrange("p (g m t) -> p g t m", t=4, m=128),
            )

        def place_weights():
            nc.scalar.copy(out=w_pad[:, 0 : 4 * NG], in_=w_sb[:].rearrange("p g t -> p (g t)"))
            bank = st_pool.tile([128, 512], F32, name="st")
            nc.tensor.transpose(bank[:, 0:128], w_pad[:], ident[:])
            nc.scalar.copy(out=w_turn[:], in_=bank[:, 0:128])
            nc.tensor.transpose(w_ps[:], w_turn[:], ident[:])

        grp = {}
        grp_g = {}
        px_q = {}
        sig = {}
        hgrp = {}
        h_q = {}
        zs = {}

        def interleave(copy, g, c, m0, m1):
            if m1 > m0:
                nt = 4 if c == 0 else T1
                copy(
                    out=grp[g][:, 2048 * c : 2048 * c + 512 * nt].rearrange("p (t m j) -> p m j t", t=nt, j=4)[:, m0:m1],
                    in_=px_raw[g][:, c].rearrange("p j (m t) -> p m j t", t=4)[:, m0:m1, :, 0:nt],
                )

        def gpsimd_share(g):
            grp_g[g] = keep.tile([128, 512 * (4 - T1)], BF16, name="grp_g", align_bytes=64)
            nc.gpsimd.tensor_scalar(
                out=grp_g[g][:].rearrange("p (t m j) -> p m j t", t=4 - T1, j=4),
                in0=px_raw[g][:, 1].rearrange("p j (m t) -> p m j t", t=4)[:, :, :, T1:4],
                scalar1=1.0,
                scalar2=0.0,
                op0=ALU.mult,
                op1=ALU.add,
            )

        def alone(copy, g, m0, m1):
            if m0 == 0:
                grp_g[g] = keep.tile([128, 512 * (4 - T1)], BF16, name="grp_g", align_bytes=64)
            if m1 > m0:
                copy(
                    out=grp_g[g][:].rearrange("p (t m j) -> p m j t", t=4 - T1, j=4)[:, m0:m1],
                    in_=px_raw[g][:, 1].rearrange("p j (m t) -> p m j t", t=4)[:, m0:m1, :, T1:4],
                )

        def start_group(g):
            grp[g] = two.tile([128, 2048 + 512 * T1], BF16, name="grp", align_bytes=64)
            px_q[g] = (
                three.tile([128, 2, 512], U32, name="pxcd", align_bytes=64),
                three.tile([128, 2, 512], U8, name="pxsc", align_bytes=64),
            )

        def quant_px(g, c):
            codes, scl = px_q[g]
            n = 512 if c == 0 else 128 * T1
            nc.vector.quantize_mx(
                out=codes[:, c, 0:n].bitcast(FP8X4),
                scales=scl[:, c, 0:n],
                in_=grp[g][:, 2048 * c : 2048 * c + 4 * n],
            )
            if c == 1:
                for a, b in G_RUNS:
                    nc.vector.quantize_mx(
                        out=codes[:, 1, n + a : n + b].bitcast(FP8X4),
                        scales=scl[:, 1, n + a : n + b],
                        in_=grp_g[g][:, 4 * a : 4 * b],
                    )

        def quant_coef():
            nc.vector.quantize_mx(out=coef_cd[:].bitcast(FP8X4), scales=coef_sc[:], in_=coef_grp[:])

        def quant_emb(c):
            nc.vector.quantize_mx(out=emb_cd[:, c, :].bitcast(FP8X4), scales=emb_sc[:, c, :], in_=emb_grp[:, c, :])

        def coarse(g, t):
            zs[g, t] = st_pool.tile([128, 512], F32, name="st")
            col = 512 * g + 128 * t
            nc.tensor.matmul_mx(
                out=zs[g, t][:],
                lhsT=proto_wd[:, 2 * col : 2 * col + 256].bitcast(FP4X4),
                lhsT_scale=pscl[:, col : col + 128],
                rhs=coef_cd[:].bitcast(FP8X4),
                rhs_scale=coef_sc[:],
                start=True,
                stop=False,
            )

        def fine(g, t):
            codes, scl = px_q[g]
            for c in range(2):
                nc.tensor.matmul_mx(
                    out=zs[g, t][:],
                    lhsT=codes[:, c, 128 * t : 128 * (t + 1)].bitcast(FP8X4),
                    lhsT_scale=scl[:, c, 128 * t : 128 * (t + 1)],
                    rhs=emb_cd[:, c, :].bitcast(FP8X4),
                    rhs_scale=emb_sc[:, c, :],
                    start=False,
                    stop=(c == 1),
                )

        def sigmoid(g, t, q0=0, q1=512):
            if t == 0:
                sig[g] = two.tile([128, 4, 512], F32, name="sig", align_bytes=64)
            nc.scalar.activation(out=sig[g][:, t, q0:q1], in_=zs[g, t][:, q0:q1], func=ACT.Sigmoid)

        def start_h(g):
            hgrp[g] = two.tile([128, 2048], BF16, name="hgrp", align_bytes=64)
            h_q[g] = (
                three.tile([128, 512], U32, name="hcd", align_bytes=64),
                three.tile([128, 512], U8, name="hsc", align_bytes=64),
            )

        def weigh(g, q0, q1):
            n = (q1 - q0) // 2
            nc.vector.tensor_tensor(
                out=hgrp[g][:, 4 * q0 : 4 * q1].rearrange("p (c i t) -> p c t i", i=2, t=4),
                in0=sig[g][:, :, q0:q1].rearrange("p t (c i) -> p c t i", i=2),
                in1=w_ps[:, 4 * g : 4 * g + 4].unsqueeze(1).unsqueeze(3).to_broadcast([128, n, 4, 2]),
                op=ALU.mult,
            )

        def quant_h(g, q0, q1):
            cd, sc = h_q[g]
            nc.vector.quantize_mx(
                out=cd[:, q0:q1].bitcast(FP8X4), scales=sc[:, q0:q1], in_=hgrp[g][:, 4 * q0 : 4 * q1]
            )

        def stage2(g, q):
            cd, sc = h_q[g]
            nc.tensor.matmul_mx(
                out=acc[q][:],
                lhsT=cd[:, 128 * q : 128 * (q + 1)].bitcast(FP8X4),
                lhsT_scale=sc[:, 128 * q : 128 * (q + 1)],
                rhs=mask_wd[:, g, :].bitcast(FP4X4),
                rhs_scale=mscl[:, g, :],
                start=(g == 0),
                stop=(g == NG - 1),
            )

        v_copy, s_copy = nc.vector.tensor_copy, nc.scalar.copy

        turn(coef_raw, 0, 0, coef_grp, s_copy)
        permute_words(0)
        permute_words(1)
        permute_words(2)
        permute_words(3)
        turn(coef_raw, 2, 0, coef_grp, s_copy)
        permute_scales(0, 2)
        permute_words(4)
        quant_coef()
        turn(emb_raw, 0, 0, emb_grp[:, 0, :], s_copy)
        turn(emb_raw, 0, 256, emb_grp[:, 1, :], v_copy)
        turn(emb_raw, 2, 0, emb_grp[:, 0, :], s_copy)
        turn(emb_raw, 2, 256, emb_grp[:, 1, :], s_copy)
        permute_words(6)
        permute_words(7)
        permute_scales(2, 4)
        permute_scales(6, 8)
        place_weights()
        for t in range(3):
            coarse(0, t)
        start_group(0)
        interleave(s_copy, 0, 0, V_SHARE[0], 128)
        permute_words(5)
        interleave(v_copy, 0, 0, 0, V_SHARE[0])
        quant_emb(0)
        quant_px(0, 0)
        quant_emb(1)
        interleave(v_copy, 0, 1, 0, V_SHARE[0])
        interleave(s_copy, 0, 1, V_SHARE[0], 128)
        alone(v_copy, 0, 0, V_SHARE[0])
        alone(s_copy, 0, V_SHARE[0], 128)
        start_group(1)
        interleave(v_copy, 1, 0, 0, V_SHARE[1])
        interleave(s_copy, 1, 0, V_SHARE[1], 128)
        quant_px(0, 1)
        interleave(v_copy, 1, 1, 0, V_SHARE[1])
        alone(v_copy, 1, 0, V_SHARE[1])
        alone(s_copy, 1, V_SHARE[1], 128)
        interleave(s_copy, 1, 1, V_SHARE[1], 128)

        for i in range(NG):
            nxt = i + 2
            if nxt < NG:
                start_group(nxt)
            if i + 1 < NG:
                quant_px(i + 1, 0)
                quant_px(i + 1, 1)
            if GFIRST <= nxt < NG:
                gpsimd_share(nxt)
            if i >= 1:
                start_h(i - 1)
                weigh(i - 1, 0, 256)
                weigh(i - 1, 256, 512)
            if nxt < NG:
                interleave(v_copy, nxt, 0, 0, V_SHARE[nxt])
            if i >= 1:
                quant_h(i - 1, 0, 256)
            if nxt < NG:
                interleave(v_copy, nxt, 1, 0, V_SHARE[nxt])
                if nxt < GFIRST:
                    alone(v_copy, nxt, 0, V_SHARE[nxt])
            if i >= 1:
                quant_h(i - 1, 256, 512)
            if i == 0:
                permute_scales(4, 6)
            last = i == NG - 1
            for t in range(4):
                if i > 0 or t == 3:
                    coarse(i, t)
                fine(i, t)
                if last and t == 3:
                    for q in range(4):
                        sigmoid(i, t, 128 * q, 128 * (q + 1))
                else:
                    sigmoid(i, t)
                if nxt < NG:
                    c, half = t // 2, t % 2
                    v = V_SHARE[nxt]
                    mid = v + (128 - v) // 2
                    lo, hi = ((v, mid), (mid, 128))[half]
                    interleave(s_copy, nxt, c, lo, hi)
                    if t == 3 and nxt < GFIRST:
                        alone(s_copy, nxt, v, 128)
                if t == 0 and i >= 2 and not last:
                    for q in range(4):
                        stage2(i - 2, q)

        g = NG - 1
        nc.scalar.activation(out=warm[:], in_=warm[:], func=ACT.Abs_reciprocal_sqrt)
        for k in (g - 2, g - 1):
            for q in range(4):
                stage2(k, q)
        start_h(g)
        for q0 in (0, 256):
            n = 128
            nc.vector.tensor_tensor(
                out=hgrp[g][:, 4 * q0 : 4 * q0 + 1024].rearrange("p (c i t) -> p c t i", i=2, t=4)[:, :, 0:3],
                in0=sig[g][:, 0:3, q0 : q0 + 256].rearrange("p t (c i) -> p c t i", i=2),
                in1=w_ps[:, 4 * g : 4 * g + 3].unsqueeze(1).unsqueeze(3).to_broadcast([128, n, 3, 2]),
                op=ALU.mult,
            )

        def weigh_last(q):
            nc.vector.tensor_scalar(
                out=hgrp[g][:, 512 * q : 512 * (q + 1)].rearrange("p (c t) -> p c t", t=4)[:, :, 3],
                in0=sig[g][:, 3, 128 * q : 128 * (q + 1)],
                scalar1=w_pad[:, 4 * g + 3 : 4 * g + 4],
                scalar2=None,
                op0=ALU.mult,
            )

        m0s = {}
        sgn = {}
        num = {}
        inv = {}

        def minus_area(q):
            m0s[q] = four.tile([128, 1], F32, name="m0")
            nc.vector.tensor_scalar(out=m0s[q][:], in0=acc[q][:, 0:1], scalar1=-1.0, scalar2=None, op0=ALU.mult)

        def sign(engine, q):
            sgn[q] = four.tile([128, 512], F32, name="sgn")
            engine.tensor_scalar(
                out=sgn[q][:], in0=area_b[:], scalar1=m0s[q][:], scalar2=0.5, op0=ALU.is_ge, op1=ALU.subtract
            )

        def root(q):
            r1 = two.tile([128, 512], F32, name="r1")
            nc.scalar.activation(
                out=r1[:], in_=area_b[:], func=ACT.Abs_reciprocal_sqrt, bias=m0s[q][:], scale=-1.0
            )
            inv[q] = r1

        def square(q):
            r2 = four.tile([128, 512], F32, name="r2")
            nc.scalar.activation(out=r2[:], in_=inv[q][:], func=ACT.Square)
            inv[q] = r2

        def signed(q):
            num[q] = four.tile([128, 512], F32, name="num")
            nc.vector.scalar_tensor_tensor(
                out=num[q][:], in0=acc[q][:], scalar=4.0, in1=sgn[q][:], op0=ALU.mult, op1=ALU.mult
            )

        def finish(q):
            res = four.tile([128, 512], F32, name="res")
            nc.vector.tensor_tensor(out=res[:], in0=num[q][:], in1=inv[q][:], op=ALU.mult)
            nc.sync.dma_start(out=out.rearrange("(p a) n -> a p n", a=4)[q], in_=res[:])

        weigh_last(0)
        weigh_last(1)
        quant_h(g, 0, 128)
        stage2(g, 0)
        weigh_last(2)
        quant_h(g, 128, 256)
        stage2(g, 1)
        weigh_last(3)
        quant_h(g, 256, 384)
        stage2(g, 2)
        minus_area(0)
        quant_h(g, 384, 512)
        stage2(g, 3)
        for q in range(4):
            if q >= 1:
                minus_area(q)
            root(q)
            square(q)
        sign(nc.vector, 0)
        sign(nc.vector, 1)
        sign(nc.gpsimd, 2)
        sign(nc.gpsimd, 3)
        signed(0)
        signed(1)
        finish(0)
        signed(2)
        finish(1)
        signed(3)
        finish(2)
        finish(3)
